import numpy as np
CORES = [78,86,94,102,110,118]
N = 6
B, TIMES = 64, 2
def setup_inputs(rng):
    return {"x": (rng.standard_normal((N, 128, B), dtype=np.float32) * (0.5 + np.abs(rng.standard_normal((1, 1, B), dtype=np.float32))) / np.float32(np.sqrt(128 * N))), "a": (rng.standard_normal((N, 128, N * 128), dtype=np.float32) / 8)}
def setup_inputs_big(rng):
    d = setup_inputs(rng)
    for k in ("a",): d[k] = (d[k].astype(np.float32) * 1048576.0).astype(d[k].dtype)
    return d
def setup_inputs_small(rng):
    d = setup_inputs(rng)
    for k in ("a",): d[k] = (d[k].astype(np.float32) * (1 / 1048576.0)).astype(d[k].dtype)
    return d
def setup_inputs_apart(rng):
    d = setup_inputs(rng)
    f = (10.0 ** rng.permutation(np.linspace(-1.5, 1.5, N))).astype(np.float32).reshape(N, 1, 1)
    for k in ("a",): d[k] = (d[k].astype(np.float32) * f).astype(d[k].dtype)
    return d
def reference(x, a):
    X, A = x.astype(np.float64), a.astype(np.float64)
    h = X
    for _ in range(TIMES):
        h = np.stack([sum(A[r][:, 128 * j:128 * j + 128].T @ h[j] for j in range(N)) for r in range(N)])
        h = h / np.sqrt((h ** 2).sum(axis=(0, 1)))
        h = h + X
    return {"y": h.astype(np.float32)}

@@ -1,0 +1,186 @@
+from concourse.bass import DstId, RemoteDMATransfer
+from concourse.mybir import AluOpType, AxisListType, ActivationFunctionType
+
+N = 6
+B = 64
+F32 = "float32"
+
+SCRATCH = {
+    "A": ("sbuf", [128, N * 128], F32),
+    "XL": ("sbuf", [128, N * B], F32),
+    "UL": ("sbuf", [128, N * B], F32),
+    "L3": ("sbuf", [128, N * 4], F32),
+    "ones": ("sbuf", [128, 128], F32),
+    "two": ("sbuf", [128, 4], F32),
+    "ident": ("sbuf", [128, 128], F32),
+    "usq": ("sbuf", [128, N * B], F32),
+    "acc": ("sbuf", [128, B], F32),
+    "wu": ("sbuf", [128, B], F32),
+    "ww": ("sbuf", [128, B], F32),
+    "Wsb": ("sbuf", [128, B], F32),
+    "tmpT": ("sbuf", [128, 128], F32),
+    "vT": ("sbuf", [128, 128], F32),
+    "diag": ("sbuf", [128, B], F32),
+    "col": ("sbuf", [128, 32], F32),
+    "junk": ("sbuf", [128, 8], F32),
+    "Ysb": ("sbuf", [128, B], F32),
+    "Ups": ("psum", [128, 512], F32),
+    "UTps": ("psum", [128, 512], F32),
+    "Wps": ("psum", [128, 512], F32),
+    "WTps": ("psum", [128, 512], F32),
+    "PQps": ("psum", [128, 512], F32),
+    "S1ps": ("psum", [128, 512], F32),
+    "Yps": ("psum", [128, 512], F32),
+}
+
+SEMAPHORES = (["ldx", "lda", "sty", "sent", "c_ones", "c_two", "c_l3", "c_id",
+               "u_mm", "u_sb", "ut_mm", "acc", "w_mm", "wu", "w_sb", "ww", "pq_mm", "pq_sb",
+               "s1_mm", "wt_mm", "r1sq", "r1", "tmpT", "vT", "p", "sq_red", "sp_red", "t", "n2", "rn2",
+               "diag", "y_mm", "y_sb"]
+              + ["x%d" % j for j in range(N)] + ["u%d" % j for j in range(N)] + ["q%d" % j for j in range(N)])
+
+
+def rank_program(g, core, T, topo):
+    r = T.rank_of(core)
+    if r is None:
+        return
+    S = T.sem
+    cores = list(T.cores)
+    Act, Op = ActivationFunctionType, AluOpType
+    out_order = [(r + k) % N for k in range(1, N)]
+    in_order = [(r - k) % N for k in range(1, N)]
+
+    mask = -1
+    for j in out_order:
+        if not topo.may_write(core, cores[j]):
+            raise ValueError("rank %d may not write to rank %d directly" % (r, j))
+        mask &= topo.mask(core, cores[j])
+    ne = bin(mask).count("1")
+
+    waited = {}
+
+    def need(q, name, sem, val=1):
+        if waited.get((name, sem), 0) < val:
+            waited[(name, sem)] = val
+            q.wait_ge(S[sem], val)
+
+    def gq(sem, val=1): need(g, "g", sem, val)
+    def tq(sem, val=1): need(g.tensor, "t", sem, val)
+    def vq(sem, val=1): need(g.vector, "v", sem, val)
+    def sq(sem, val=1): need(g.scalar, "s", sem, val)
+    def yq(sem, val=1): need(g.sync, "y", sem, val)
+
+    def sl(j, w=B):
+        return slice(j * w, (j + 1) * w)
+
+    def spread(ap, sem):
+        ids = [DstId(rid=topo.addr(cores[j])[0], pnc=topo.addr(cores[j])[1]) for j in out_order]
+        g.remote_dma_fused([RemoteDMATransfer(dst_ids=ids, dma_engine_mask=mask, remote_sem=S[sem],
+                                              srcs=[ap], dsts=[ap for _ in out_order], alu_op=0)],
+                           local_sem=S.sent)
+
+    H = slice(0, B)
+    c_r1sq, c_r1, c_sq, c_sp, c_t, c_n2, c_rn2 = [T.col[H, 4 * i:4 * i + 1] for i in range(7)]
+    one = T.ones[:, 0:1]
+    xr, ur, ar = T.XL[:, sl(r)], T.UL[:, sl(r)], T.A[:, sl(r, 128)]
+
+    g.sync.dma_start(xr, T.x[:]).then_inc(S.ldx, 16)
+    g.sync.dma_start(T.A[:], T.a[:]).then_inc(S.lda, 16)
+    g.vector.memset(T.ones[:], 1.0).then_inc(S.c_ones, 1)
+    g.vector.memset(T.two[:], 2.0).then_inc(S.c_two, 1)
+    g.vector.memset(T.L3[:, sl(r, 4)], 0.0).then_inc(S.c_l3, 1)
+    gq("c_ones")
+    g.affine_select(T.ident[:], T.ones[:], [[-1, 128]], Op.is_equal, 0.0, 0, 1).then_inc(S.c_id, 1)
+
+    gq("ldx", 16)
+    spread(xr, "x%d" % r)
+    tq("ldx", 16)
+    tq("lda", 16)
+    g.tensor.matmul(T.Ups[:, H], ar, xr, True, False)
+    for k, j in enumerate(in_order):
+        tq("x%d" % j, ne)
+        mm = g.tensor.matmul(T.Ups[:, H], T.A[:, sl(j, 128)], T.XL[:, sl(j)], False, k == N - 2)
+    mm.then_inc(S.u_mm, 1)
+    vq("u_mm")
+    g.vector.tensor_copy(ur, T.Ups[:, H]).then_inc(S.u_sb, 1)
+
+    gq("u_sb")
+    spread(ur, "u%d" % r)
+    tq("u_sb")
+    g.tensor.matmul(T.Wps[:, H], ar, ur, True, False)
+    tq("c_id")
+    g.tensor.matmul(T.UTps[H, 0:128], ur, T.ident[:], True, True).then_inc(S.ut_mm, 1)
+    sq("u_sb")
+    g.scalar.activation(T.acc[:], ur, Act.Square).then_inc(S["q%d" % r], 1)
+    vq("q%d" % r)
+    for k, j in enumerate(in_order):
+        tq("u%d" % j, ne)
+        mm = g.tensor.matmul(T.Wps[:, H], T.A[:, sl(j, 128)], T.UL[:, sl(j)], False, k == N - 2)
+        sq("u%d" % j, ne)
+        g.scalar.activation(T.usq[:, sl(j)], T.UL[:, sl(j)], Act.Square).then_inc(S["q%d" % j], 1)
+        vq("q%d" % j)
+        vq("acc", k)
+        g.vector.tensor_tensor(T.acc[:], T.acc[:], T.usq[:, sl(j)], Op.add).then_inc(S.acc, 1)
+    mm.then_inc(S.w_mm, 1)
+
+    vq("w_mm")
+    vq("u_sb")
+    g.vector.tensor_tensor(T.wu[:], T.Wps[:, H], ur, Op.mult).then_inc(S.wu, 1)
+    g.vector.tensor_copy(T.Wsb[:], T.Wps[:, H]).then_inc(S.w_sb, 1)
+    sq("w_sb")
+    g.scalar.activation(T.ww[:], T.Wsb[:], Act.Square).then_inc(S.ww, 1)
+    tq("c_two")
+    tq("c_ones")
+    tq("wu")
+    g.tensor.matmul(T.PQps[H, 0:1], T.wu[:], T.two[:, 0:1], True, True).then_inc(S.pq_mm, 1)
+    tq("ww")
+    g.tensor.matmul(T.PQps[H, 1:2], T.ww[:], one, True, True).then_inc(S.pq_mm, 1)
+    vq("pq_mm", 2)
+    vq("c_l3")
+    g.vector.tensor_copy(T.L3[H, 4 * r:4 * r + 2], T.PQps[H, 0:2]).then_inc(S.pq_sb, 1)
+
+    gq("c_l3")
+    gq("pq_sb")
+    spread(T.L3[:, 4 * r:4 * r + 2], "p")
+
+    tq("acc", N - 1)
+    g.tensor.matmul(T.S1ps[H, 0:1], T.acc[:], one, True, True).then_inc(S.s1_mm, 1)
+    tq("w_sb")
+    g.tensor.matmul(T.WTps[H, 0:128], T.Wsb[:], T.ident[:], True, True).then_inc(S.wt_mm, 1)
+    vq("s1_mm")
+    g.vector.reciprocal(c_r1sq, T.S1ps[H, 0:1]).then_inc(S.r1sq, 1)
+    sq("r1sq")
+    g.scalar.activation(c_r1, c_r1sq, Act.Sqrt).then_inc(S.r1, 1)
+    vq("r1")
+    vq("wt_mm")
+    g.vector.tensor_scalar(T.tmpT[H, :], T.WTps[H, 0:128], c_r1, None, Op.mult).then_inc(S.tmpT, 1)
+    vq("tmpT")
+    vq("ut_mm")
+    g.vector.tensor_tensor(T.vT[H, :], T.tmpT[H, :], T.UTps[H, 0:128], Op.add).then_inc(S.vT, 1)
+
+    vq("p", (N - 1) * ne)
+    vq("pq_sb")
+    g.vector.tensor_reduce(c_sq, T.L3[H, 0:4 * N:4], AxisListType.X, Op.add).then_inc(S.sq_red, 1)
+    sq("p", (N - 1) * ne)
+    sq("pq_sb")
+    g.scalar.activation(T.junk[H, 0:N], T.L3[H, 1:4 * N:4], Act.Identity, accum_out=c_sp).then_inc(S.sp_red, 1)
+    vq("sq_red")
+    g.vector.tensor_scalar(c_t, c_sq, c_r1, T.S1ps[H, 0:1], Op.mult, Op.add).then_inc(S.t, 1)
+    sq("t")
+    sq("sp_red")
+    g.scalar.activation(c_n2, c_sp, Act.Sqrt, bias=c_t, scale=c_r1sq).then_inc(S.n2, 1)
+    vq("n2")
+    g.vector.reciprocal(c_rn2, c_n2).then_inc(S.rn2, 1)
+    vq("rn2")
+    vq("c_id")
+    g.vector.tensor_scalar(T.diag[H, :], T.ident[H, H], c_rn2, None, Op.mult).then_inc(S.diag, 1)
+    tq("diag")
+    tq("vT")
+    g.tensor.matmul(T.Yps[:, H], T.vT[H, :], T.diag[H, :], True, True).then_inc(S.y_mm, 1)
+    vq("y_mm")
+    vq("ldx", 16)
+    g.vector.tensor_tensor(T.Ysb[:], T.Yps[:, H], xr, Op.add).then_inc(S.y_sb, 1)
+    yq("y_sb")
+    g.sync.dma_start(T.y[:], T.Ysb[:]).then_inc(S.sty, 16)
+    yq("sty", 16)
+    gq("sent", 3 * ne)

@@ -4,12 +4,15 @@ from concourse.mybir import AluOpType, AxisListType, ActivationFunctionType
 N = 6
 B = 64
 F32 = "float32"
+W3 = 4 + 2 * (N - 1)
 
 SCRATCH = {
     "A": ("sbuf", [128, N * 128], F32),
     "XL": ("sbuf", [128, N * B], F32),
     "UL": ("sbuf", [128, N * B], F32),
-    "L3": ("sbuf", [128, N * 4], F32),
+    "L3": ("sbuf", [128, 16], F32),
+    "D0": ("sbuf", [128, 16], F32),
+    "sc": ("sbuf", [128, 16], F32),
     "ones": ("sbuf", [128, 128], F32),
     "two": ("sbuf", [128, 4], F32),
     "ident": ("sbuf", [128, 128], F32),
@@ -20,24 +23,54 @@ SCRATCH = {
     "Wsb": ("sbuf", [128, B], F32),
     "tmpT": ("sbuf", [128, 128], F32),
     "vT": ("sbuf", [128, 128], F32),
+    "dS1": ("sbuf", [128, B], F32),
     "diag": ("sbuf", [128, B], F32),
     "col": ("sbuf", [128, 32], F32),
-    "junk": ("sbuf", [128, 8], F32),
     "Ysb": ("sbuf", [128, B], F32),
     "Ups": ("psum", [128, 512], F32),
     "UTps": ("psum", [128, 512], F32),
     "Wps": ("psum", [128, 512], F32),
     "WTps": ("psum", [128, 512], F32),
     "PQps": ("psum", [128, 512], F32),
+    "S0ps": ("psum", [128, 512], F32),
     "S1ps": ("psum", [128, 512], F32),
     "Yps": ("psum", [128, 512], F32),
 }
 
 SEMAPHORES = (["ldx", "lda", "sty", "sent", "c_ones", "c_two", "c_l3", "c_id",
                "u_mm", "u_sb", "ut_mm", "acc", "w_mm", "wu", "w_sb", "ww", "pq_mm", "pq_sb",
-               "s1_mm", "wt_mm", "r1sq", "r1", "tmpT", "vT", "p", "sq_red", "sp_red", "t", "n2", "rn2",
-               "diag", "y_mm", "y_sb"]
+               "s0_mm", "sig0", "rho0", "s1_mm", "wt_mm", "q", "d0a", "r1", "d0b", "ds1", "tmpT", "vT",
+               "p", "scan", "rc", "diag", "y_mm", "y_sb"]
               + ["x%d" % j for j in range(N)] + ["u%d" % j for j in range(N)] + ["q%d" % j for j in range(N)])
+
+
+def steps_of(cores, topo):
+    def far(s, j):
+        cs, cj = topo.chip(cores[s]), topo.chip(cores[j])
+        return 0 if topo.mates(cs, cj) else (1 if topo.same_plane(cs, cj) else 2)
+
+    g0 = [j for j in range(N) if j == 0 or topo.same_plane(topo.chip(cores[0]), topo.chip(cores[j]))]
+    g1 = [j for j in range(N) if j not in g0]
+    h = len(g0)
+    if len(g1) != h:
+        raise ValueError("the ranks don't fall into two planes of equal size")
+    cross = []
+    for s in range(h):
+        d = {}
+        for i in range(h):
+            a, b = g0[i], g1[(i + s) % h]
+            d[a] = b
+            d[b] = a
+        cross.append(d)
+    cross.sort(key=lambda d: -sum(far(a, d[a]) for a in d))
+    inside = []
+    for s in range(1, h):
+        d = {}
+        for grp in (g0, g1):
+            for i in range(h):
+                d[grp[i]] = grp[(i + s) % h]
+        inside.append(d)
+    return cross + inside
 
 
 def rank_program(g, core, T, topo):
@@ -47,8 +80,10 @@ def rank_program(g, core, T, topo):
     S = T.sem
     cores = list(T.cores)
     Act, Op = ActivationFunctionType, AluOpType
-    out_order = [(r + k) % N for k in range(1, N)]
-    in_order = [(r - k) % N for k in range(1, N)]
+
+    steps = steps_of(cores, topo)
+    out_order = [d[r] for d in steps]
+    in_order = [[j for j in d if d[j] == r][0] for d in steps]
 
     mask = -1
     for j in out_order:
@@ -73,27 +108,28 @@ def rank_program(g, core, T, topo):
     def sl(j, w=B):
         return slice(j * w, (j + 1) * w)
 
-    def spread(ap, sem):
+    def spread(src, dsts, sem):
         ids = [DstId(rid=topo.addr(cores[j])[0], pnc=topo.addr(cores[j])[1]) for j in out_order]
         g.remote_dma_fused([RemoteDMATransfer(dst_ids=ids, dma_engine_mask=mask, remote_sem=S[sem],
-                                              srcs=[ap], dsts=[ap for _ in out_order], alu_op=0)],
+                                              srcs=[src], dsts=dsts, alu_op=0)],
                            local_sem=S.sent)
 
     H = slice(0, B)
-    c_r1sq, c_r1, c_sq, c_sp, c_t, c_n2, c_rn2 = [T.col[H, 4 * i:4 * i + 1] for i in range(7)]
+    c_sig0, c_rho0, c_q, c_r1, c_rc = [T.col[H, 4 * i:4 * i + 1] for i in range(5)]
     one = T.ones[:, 0:1]
     xr, ur, ar = T.XL[:, sl(r)], T.UL[:, sl(r)], T.A[:, sl(r, 128)]
+    s1 = T.S1ps[H, 0:1]
 
     g.sync.dma_start(xr, T.x[:]).then_inc(S.ldx, 16)
     g.sync.dma_start(T.A[:], T.a[:]).then_inc(S.lda, 16)
     g.vector.memset(T.ones[:], 1.0).then_inc(S.c_ones, 1)
     g.vector.memset(T.two[:], 2.0).then_inc(S.c_two, 1)
-    g.vector.memset(T.L3[:, sl(r, 4)], 0.0).then_inc(S.c_l3, 1)
-    gq("c_ones")
-    g.affine_select(T.ident[:], T.ones[:], [[-1, 128]], Op.is_equal, 0.0, 0, 1).then_inc(S.c_id, 1)
+    g.vector.memset(T.L3[:, 0:4], 0.0).then_inc(S.c_l3, 1)
 
     gq("ldx", 16)
-    spread(xr, "x%d" % r)
+    spread(xr, [xr for _ in out_order], "x%d" % r)
+    gq("c_ones")
+    g.affine_select(T.ident[:], T.ones[:], [[-1, 128]], Op.is_equal, 0.0, 0, 1).then_inc(S.c_id, 1)
     tq("ldx", 16)
     tq("lda", 16)
     g.tensor.matmul(T.Ups[:, H], ar, xr, True, False)
@@ -105,75 +141,94 @@ def rank_program(g, core, T, topo):
     g.vector.tensor_copy(ur, T.Ups[:, H]).then_inc(S.u_sb, 1)
 
     gq("u_sb")
-    spread(ur, "u%d" % r)
+    spread(ur, [ur for _ in out_order], "u%d" % r)
+    sq("u_sb")
+    g.scalar.activation(T.usq[:, sl(r)], ur, Act.Square).then_inc(S["q%d" % r], 1)
+    tq("q%d" % r)
+    tq("c_ones")
+    g.tensor.matmul(T.S0ps[H, 0:1], T.usq[:, sl(r)], one, True, True).then_inc(S.s0_mm, 1)
     tq("u_sb")
     g.tensor.matmul(T.Wps[:, H], ar, ur, True, False)
     tq("c_id")
     g.tensor.matmul(T.UTps[H, 0:128], ur, T.ident[:], True, True).then_inc(S.ut_mm, 1)
-    sq("u_sb")
-    g.scalar.activation(T.acc[:], ur, Act.Square).then_inc(S["q%d" % r], 1)
+    sq("s0_mm")
+    g.scalar.activation(c_sig0, T.S0ps[H, 0:1], Act.Sqrt).then_inc(S.sig0, 1)
+    vq("s0_mm")
+    vq("sig0")
+    g.vector.reciprocal(c_rho0, T.S0ps[H, 0:1]).then_inc(S.rho0, 1)
     vq("q%d" % r)
+
+    def add_sq(k, j):
+        vq("q%d" % j)
+        vq("acc", k)
+        g.vector.tensor_tensor(T.acc[:], T.usq[:, sl(r)] if k == 0 else T.acc[:], T.usq[:, sl(j)],
+                               Op.add).then_inc(S.acc, 1)
+
     for k, j in enumerate(in_order):
         tq("u%d" % j, ne)
         mm = g.tensor.matmul(T.Wps[:, H], T.A[:, sl(j, 128)], T.UL[:, sl(j)], False, k == N - 2)
         sq("u%d" % j, ne)
         g.scalar.activation(T.usq[:, sl(j)], T.UL[:, sl(j)], Act.Square).then_inc(S["q%d" % j], 1)
-        vq("q%d" % j)
-        vq("acc", k)
-        g.vector.tensor_tensor(T.acc[:], T.acc[:], T.usq[:, sl(j)], Op.add).then_inc(S.acc, 1)
+        if k < N - 2:
+            add_sq(k, j)
     mm.then_inc(S.w_mm, 1)
 
     vq("w_mm")
     vq("u_sb")
     g.vector.tensor_tensor(T.wu[:], T.Wps[:, H], ur, Op.mult).then_inc(S.wu, 1)
-    g.vector.tensor_copy(T.Wsb[:], T.Wps[:, H]).then_inc(S.w_sb, 1)
-    sq("w_sb")
-    g.scalar.activation(T.ww[:], T.Wsb[:], Act.Square).then_inc(S.ww, 1)
+    sq("w_mm")
+    sq("wu")
+    g.scalar.activation(T.ww[:], T.Wps[:, H], Act.Square).then_inc(S.ww, 1)
     tq("c_two")
-    tq("c_ones")
     tq("wu")
     g.tensor.matmul(T.PQps[H, 0:1], T.wu[:], T.two[:, 0:1], True, True).then_inc(S.pq_mm, 1)
     tq("ww")
     g.tensor.matmul(T.PQps[H, 1:2], T.ww[:], one, True, True).then_inc(S.pq_mm, 1)
+    vq("ww")
+    g.vector.tensor_copy(T.Wsb[:], T.Wps[:, H]).then_inc(S.w_sb, 1)
     vq("pq_mm", 2)
     vq("c_l3")
-    g.vector.tensor_copy(T.L3[H, 4 * r:4 * r + 2], T.PQps[H, 0:2]).then_inc(S.pq_sb, 1)
+    g.vector.tensor_copy(T.L3[H, 0:2], T.PQps[H, 0:2]).then_inc(S.pq_sb, 1)
 
     gq("c_l3")
     gq("pq_sb")
-    spread(T.L3[:, 4 * r:4 * r + 2], "p")
+    place = [2 + 2 * ((j - r) % N) for j in out_order]
+    spread(T.L3[:, 0:2], [T.L3[:, c:c + 2] for c in place], "p")
 
+    add_sq(N - 2, in_order[N - 2])
     tq("acc", N - 1)
-    g.tensor.matmul(T.S1ps[H, 0:1], T.acc[:], one, True, True).then_inc(S.s1_mm, 1)
+    g.tensor.matmul(s1, T.acc[:], one, True, True).then_inc(S.s1_mm, 1)
     tq("w_sb")
     g.tensor.matmul(T.WTps[H, 0:128], T.Wsb[:], T.ident[:], True, True).then_inc(S.wt_mm, 1)
+    sq("s1_mm")
+    sq("rho0")
+    g.scalar.activation(c_q, s1, Act.Sqrt, scale=c_rho0).then_inc(S.q, 1)
+    vq("q")
     vq("s1_mm")
-    g.vector.reciprocal(c_r1sq, T.S1ps[H, 0:1]).then_inc(S.r1sq, 1)
-    sq("r1sq")
-    g.scalar.activation(c_r1, c_r1sq, Act.Sqrt).then_inc(S.r1, 1)
+    vq("c_ones")
+    g.vector.tensor_scalar(T.D0[H, 0:W3], T.ones[H, 0:W3], c_q, c_sig0, Op.mult, Op.mult).then_inc(S.d0a, 1)
+    vq("d0a")
+    g.vector.reciprocal(c_r1, T.D0[H, 1:2]).then_inc(S.r1, 1)
+    sq("r1")
+    sq("wt_mm")
+    g.scalar.activation(T.tmpT[H, :], T.WTps[H, 0:128], Act.Copy, scale=c_r1).then_inc(S.tmpT, 1)
     vq("r1")
-    vq("wt_mm")
-    g.vector.tensor_scalar(T.tmpT[H, :], T.WTps[H, 0:128], c_r1, None, Op.mult).then_inc(S.tmpT, 1)
+    g.vector.tensor_scalar(T.D0[H, 2:W3:2], T.ones[H, 0:(W3 - 2) // 2], c_r1, None, Op.mult).then_inc(S.d0b, 1)
+    vq("c_id")
+    g.vector.tensor_scalar(T.dS1[H, :], T.ident[H, H], s1, None, Op.mult).then_inc(S.ds1, 1)
     vq("tmpT")
     vq("ut_mm")
     g.vector.tensor_tensor(T.vT[H, :], T.tmpT[H, :], T.UTps[H, 0:128], Op.add).then_inc(S.vT, 1)
 
     vq("p", (N - 1) * ne)
     vq("pq_sb")
-    g.vector.tensor_reduce(c_sq, T.L3[H, 0:4 * N:4], AxisListType.X, Op.add).then_inc(S.sq_red, 1)
-    sq("p", (N - 1) * ne)
-    sq("pq_sb")
-    g.scalar.activation(T.junk[H, 0:N], T.L3[H, 1:4 * N:4], Act.Identity, accum_out=c_sp).then_inc(S.sp_red, 1)
-    vq("sq_red")
-    g.vector.tensor_scalar(c_t, c_sq, c_r1, T.S1ps[H, 0:1], Op.mult, Op.add).then_inc(S.t, 1)
-    sq("t")
-    sq("sp_red")
-    g.scalar.activation(c_n2, c_sp, Act.Sqrt, bias=c_t, scale=c_r1sq).then_inc(S.n2, 1)
-    vq("n2")
-    g.vector.reciprocal(c_rn2, c_n2).then_inc(S.rn2, 1)
-    vq("rn2")
-    vq("c_id")
-    g.vector.tensor_scalar(T.diag[H, :], T.ident[H, H], c_rn2, None, Op.mult).then_inc(S.diag, 1)
+    vq("d0b")
+    g.vector.tensor_tensor_scan(T.sc[H, 0:W3], T.D0[H, 0:W3], T.L3[H, 0:W3], s1, Op.mult, Op.add).then_inc(S.scan, 1)
+    vq("scan")
+    g.vector.reciprocal(c_rc, T.sc[H, W3 - 1:W3]).then_inc(S.rc, 1)
+    sq("rc")
+    sq("ds1")
+    g.scalar.activation(T.diag[H, :], T.dS1[H, :], Act.Sqrt, scale=c_rc).then_inc(S.diag, 1)
     tq("diag")
     tq("vT")
     g.tensor.matmul(T.Yps[:, H], T.vT[H, :], T.diag[H, :], True, True).then_inc(S.y_mm, 1)

from concourse.bass import DstId, RemoteDMATransfer
from concourse.mybir import AluOpType, AxisListType, ActivationFunctionType

N = 6
B = 64
F32 = "float32"
W3 = 4 + 2 * (N - 1)

SCRATCH = {
    "A": ("sbuf", [128, N * 128], F32),
    "XL": ("sbuf", [128, N * B], F32),
    "UL": ("sbuf", [128, N * B], F32),
    "L3": ("sbuf", [128, 16], F32),
    "D0": ("sbuf", [128, 16], F32),
    "sc": ("sbuf", [128, 16], F32),
    "ones": ("sbuf", [128, 128], F32),
    "two": ("sbuf", [128, 4], F32),
    "ident": ("sbuf", [128, 128], F32),
    "usq": ("sbuf", [128, N * B], F32),
    "acc": ("sbuf", [128, B], F32),
    "wu": ("sbuf", [128, B], F32),
    "ww": ("sbuf", [128, B], F32),
    "Wsb": ("sbuf", [128, B], F32),
    "tmpT": ("sbuf", [128, 128], F32),
    "vT": ("sbuf", [128, 128], F32),
    "dS1": ("sbuf", [128, B], F32),
    "diag": ("sbuf", [128, B], F32),
    "col": ("sbuf", [128, 32], F32),
    "Ysb": ("sbuf", [128, B], F32),
    "Ups": ("psum", [128, 512], F32),
    "UTps": ("psum", [128, 512], F32),
    "Wps": ("psum", [128, 512], F32),
    "WTps": ("psum", [128, 512], F32),
    "PQps": ("psum", [128, 512], F32),
    "S0ps": ("psum", [128, 512], F32),
    "S1ps": ("psum", [128, 512], F32),
    "Yps": ("psum", [128, 512], F32),
}

SEMAPHORES = (["ldx", "lda", "sty", "sent", "c_ones", "c_two", "c_l3", "c_id",
               "u_mm", "u_sb", "ut_mm", "acc", "w_mm", "wu", "w_sb", "ww", "pq_mm", "pq_sb",
               "s0_mm", "sig0", "rho0", "s1_mm", "wt_mm", "q", "d0a", "r1", "d0b", "ds1", "tmpT", "vT",
               "p", "scan", "rc", "diag", "y_mm", "y_sb"]
              + ["x%d" % j for j in range(N)] + ["u%d" % j for j in range(N)] + ["q%d" % j for j in range(N)])


def steps_of(cores, topo):
    def far(s, j):
        cs, cj = topo.chip(cores[s]), topo.chip(cores[j])
        return 0 if topo.mates(cs, cj) else (1 if topo.same_plane(cs, cj) else 2)

    g0 = [j for j in range(N) if j == 0 or topo.same_plane(topo.chip(cores[0]), topo.chip(cores[j]))]
    g1 = [j for j in range(N) if j not in g0]
    h = len(g0)
    if len(g1) != h:
        raise ValueError("the ranks don't fall into two planes of equal size")
    cross = []
    for s in range(h):
        d = {}
        for i in range(h):
            a, b = g0[i], g1[(i + s) % h]
            d[a] = b
            d[b] = a
        cross.append(d)
    cross.sort(key=lambda d: -sum(far(a, d[a]) for a in d))
    inside = []
    for s in range(1, h):
        d = {}
        for grp in (g0, g1):
            for i in range(h):
                d[grp[i]] = grp[(i + s) % h]
        inside.append(d)
    return cross + inside


def rank_program(g, core, T, topo):
    r = T.rank_of(core)
    if r is None:
        return
    S = T.sem
    cores = list(T.cores)
    Act, Op = ActivationFunctionType, AluOpType

    steps = steps_of(cores, topo)
    out_order = [d[r] for d in steps]
    in_order = [[j for j in d if d[j] == r][0] for d in steps]

    mask = -1
    for j in out_order:
        if not topo.may_write(core, cores[j]):
            raise ValueError("rank %d may not write to rank %d directly" % (r, j))
        mask &= topo.mask(core, cores[j])
    ne = bin(mask).count("1")

    waited = {}

    def need(q, name, sem, val=1):
        if waited.get((name, sem), 0) < val:
            waited[(name, sem)] = val
            q.wait_ge(S[sem], val)

    def gq(sem, val=1): need(g, "g", sem, val)
    def tq(sem, val=1): need(g.tensor, "t", sem, val)
    def vq(sem, val=1): need(g.vector, "v", sem, val)
    def sq(sem, val=1): need(g.scalar, "s", sem, val)
    def yq(sem, val=1): need(g.sync, "y", sem, val)

    def sl(j, w=B):
        return slice(j * w, (j + 1) * w)

    def spread(src, dsts, sem):
        ids = [DstId(rid=topo.addr(cores[j])[0], pnc=topo.addr(cores[j])[1]) for j in out_order]
        g.remote_dma_fused([RemoteDMATransfer(dst_ids=ids, dma_engine_mask=mask, remote_sem=S[sem],
                                              srcs=[src], dsts=dsts, alu_op=0)],
                           local_sem=S.sent)

    H = slice(0, B)
    c_sig0, c_rho0, c_q, c_r1, c_rc = [T.col[H, 4 * i:4 * i + 1] for i in range(5)]
    one = T.ones[:, 0:1]
    xr, ur, ar = T.XL[:, sl(r)], T.UL[:, sl(r)], T.A[:, sl(r, 128)]
    s1 = T.S1ps[H, 0:1]

    g.sync.dma_start(xr, T.x[:]).then_inc(S.ldx, 16)
    g.sync.dma_start(T.A[:], T.a[:]).then_inc(S.lda, 16)
    g.vector.memset(T.ones[:], 1.0).then_inc(S.c_ones, 1)
    g.vector.memset(T.two[:], 2.0).then_inc(S.c_two, 1)
    g.vector.memset(T.L3[:, 0:4], 0.0).then_inc(S.c_l3, 1)

    gq("ldx", 16)
    spread(xr, [xr for _ in out_order], "x%d" % r)
    gq("c_ones")
    g.affine_select(T.ident[:], T.ones[:], [[-1, 128]], Op.is_equal, 0.0, 0, 1).then_inc(S.c_id, 1)
    tq("ldx", 16)
    tq("lda", 16)
    g.tensor.matmul(T.Ups[:, H], ar, xr, True, False)
    for k, j in enumerate(in_order):
        tq("x%d" % j, ne)
        mm = g.tensor.matmul(T.Ups[:, H], T.A[:, sl(j, 128)], T.XL[:, sl(j)], False, k == N - 2)
    mm.then_inc(S.u_mm, 1)
    vq("u_mm")
    g.vector.tensor_copy(ur, T.Ups[:, H]).then_inc(S.u_sb, 1)

    gq("u_sb")
    spread(ur, [ur for _ in out_order], "u%d" % r)
    sq("u_sb")
    g.scalar.activation(T.usq[:, sl(r)], ur, Act.Square).then_inc(S["q%d" % r], 1)
    tq("q%d" % r)
    tq("c_ones")
    g.tensor.matmul(T.S0ps[H, 0:1], T.usq[:, sl(r)], one, True, True).then_inc(S.s0_mm, 1)
    tq("u_sb")
    g.tensor.matmul(T.Wps[:, H], ar, ur, True, False)
    tq("c_id")
    g.tensor.matmul(T.UTps[H, 0:128], ur, T.ident[:], True, True).then_inc(S.ut_mm, 1)
    sq("s0_mm")
    g.scalar.activation(c_sig0, T.S0ps[H, 0:1], Act.Sqrt).then_inc(S.sig0, 1)
    vq("s0_mm")
    vq("sig0")
    g.vector.reciprocal(c_rho0, T.S0ps[H, 0:1]).then_inc(S.rho0, 1)
    vq("q%d" % r)

    def add_sq(k, j):
        vq("q%d" % j)
        vq("acc", k)
        g.vector.tensor_tensor(T.acc[:], T.usq[:, sl(r)] if k == 0 else T.acc[:], T.usq[:, sl(j)],
                               Op.add).then_inc(S.acc, 1)

    for k, j in enumerate(in_order):
        tq("u%d" % j, ne)
        mm = g.tensor.matmul(T.Wps[:, H], T.A[:, sl(j, 128)], T.UL[:, sl(j)], False, k == N - 2)
        sq("u%d" % j, ne)
        g.scalar.activation(T.usq[:, sl(j)], T.UL[:, sl(j)], Act.Square).then_inc(S["q%d" % j], 1)
        if k < N - 2:
            add_sq(k, j)
    mm.then_inc(S.w_mm, 1)

    vq("w_mm")
    vq("u_sb")
    g.vector.tensor_tensor(T.wu[:], T.Wps[:, H], ur, Op.mult).then_inc(S.wu, 1)
    sq("w_mm")
    sq("wu")
    g.scalar.activation(T.ww[:], T.Wps[:, H], Act.Square).then_inc(S.ww, 1)
    tq("c_two")
    tq("wu")
    g.tensor.matmul(T.PQps[H, 0:1], T.wu[:], T.two[:, 0:1], True, True).then_inc(S.pq_mm, 1)
    tq("ww")
    g.tensor.matmul(T.PQps[H, 1:2], T.ww[:], one, True, True).then_inc(S.pq_mm, 1)
    vq("ww")
    g.vector.tensor_copy(T.Wsb[:], T.Wps[:, H]).then_inc(S.w_sb, 1)
    vq("pq_mm", 2)
    vq("c_l3")
    g.vector.tensor_copy(T.L3[H, 0:2], T.PQps[H, 0:2]).then_inc(S.pq_sb, 1)

    gq("c_l3")
    gq("pq_sb")
    place = [2 + 2 * ((j - r) % N) for j in out_order]
    spread(T.L3[:, 0:2], [T.L3[:, c:c + 2] for c in place], "p")

    add_sq(N - 2, in_order[N - 2])
    tq("acc", N - 1)
    g.tensor.matmul(s1, T.acc[:], one, True, True).then_inc(S.s1_mm, 1)
    tq("w_sb")
    g.tensor.matmul(T.WTps[H, 0:128], T.Wsb[:], T.ident[:], True, True).then_inc(S.wt_mm, 1)
    sq("s1_mm")
    sq("rho0")
    g.scalar.activation(c_q, s1, Act.Sqrt, scale=c_rho0).then_inc(S.q, 1)
    vq("q")
    vq("s1_mm")
    vq("c_ones")
    g.vector.tensor_scalar(T.D0[H, 0:W3], T.ones[H, 0:W3], c_q, c_sig0, Op.mult, Op.mult).then_inc(S.d0a, 1)
    vq("d0a")
    g.vector.reciprocal(c_r1, T.D0[H, 1:2]).then_inc(S.r1, 1)
    sq("r1")
    sq("wt_mm")
    g.scalar.activation(T.tmpT[H, :], T.WTps[H, 0:128], Act.Copy, scale=c_r1).then_inc(S.tmpT, 1)
    vq("r1")
    g.vector.tensor_scalar(T.D0[H, 2:W3:2], T.ones[H, 0:(W3 - 2) // 2], c_r1, None, Op.mult).then_inc(S.d0b, 1)
    vq("c_id")
    g.vector.tensor_scalar(T.dS1[H, :], T.ident[H, H], s1, None, Op.mult).then_inc(S.ds1, 1)
    vq("tmpT")
    vq("ut_mm")
    g.vector.tensor_tensor(T.vT[H, :], T.tmpT[H, :], T.UTps[H, 0:128], Op.add).then_inc(S.vT, 1)

    vq("p", (N - 1) * ne)
    vq("pq_sb")
    vq("d0b")
    g.vector.tensor_tensor_scan(T.sc[H, 0:W3], T.D0[H, 0:W3], T.L3[H, 0:W3], s1, Op.mult, Op.add).then_inc(S.scan, 1)
    vq("scan")
    g.vector.reciprocal(c_rc, T.sc[H, W3 - 1:W3]).then_inc(S.rc, 1)
    sq("rc")
    sq("ds1")
    g.scalar.activation(T.diag[H, :], T.dS1[H, :], Act.Sqrt, scale=c_rc).then_inc(S.diag, 1)
    tq("diag")
    tq("vT")
    g.tensor.matmul(T.Yps[:, H], T.vT[H, :], T.diag[H, :], True, True).then_inc(S.y_mm, 1)
    vq("y_mm")
    vq("ldx", 16)
    g.vector.tensor_tensor(T.Ysb[:], T.Yps[:, H], xr, Op.add).then_inc(S.y_sb, 1)
    yq("y_sb")
    g.sync.dma_start(T.y[:], T.Ysb[:]).then_inc(S.sty, 16)
    yq("sty", 16)
    gq("sent", 3 * ne)
